import numpy as np
CORES = [4,20,36,44,92,100,108,116,3,19,35,43,91,99,107,115]
N = 16
TIMES = 2
def setup_inputs(rng):
    x = (rng.standard_normal((N, 128, 128), dtype=np.float32) / np.float32(np.sqrt(512 * N)))
    return {"x": x, "xt": x.transpose(0, 2, 1).copy()}
def setup_inputs_big(rng):
    d = setup_inputs(rng)
    for k in ("x", "xt"): d[k] = (d[k].astype(np.float32) * 1024.0).astype(d[k].dtype)
    return d
def setup_inputs_small(rng):
    d = setup_inputs(rng)
    for k in ("x", "xt"): d[k] = (d[k].astype(np.float32) * (1 / 1024.0)).astype(d[k].dtype)
    return d
def setup_inputs_apart(rng):
    d = setup_inputs(rng)
    f = (10.0 ** rng.permutation(np.linspace(-1.5, 1.5, N))).astype(np.float32).reshape(N, 1, 1)
    for k in ("x", "xt"): d[k] = (d[k].astype(np.float32) * f).astype(d[k].dtype)
    return d
def reference(x, xt):
    X = list(x.astype(np.float64))
    for _ in range(TIMES):
        G = sum(a.T @ a for a in X)
        X = [1.5 * a - 0.5 * (a @ G) for a in X]
    return {"y": np.stack(X).astype(np.float32)}

@@ -1,0 +1,158 @@
+from concourse.bass import DstId, RemoteDMATransfer
+from concourse.mybir import AluOpType
+
+D = 128
+COEF = (2.25, -2.4375, 1.6875, -0.5625, 0.0625)
+HELPERS = 2
+RANK_SHARE = 2
+NCHIPS = 8
+
+SCRATCH = {
+    "xs": ("sbuf", [D, D], "float32"),
+    "xts": ("sbuf", [D, D], "float32"),
+    "cst": ("sbuf", [D, 5 * D], "float32"),
+    "sx": ("sbuf", [D, 5 * D], "float32"),
+    "pair": ("sbuf", [D, 2 * D], "float32"),
+    "land": ("sbuf", [D, NCHIPS * D], "float32"),
+    "gs": ("sbuf", [D, D], "float32"),
+    "g2s": ("sbuf", [D, D], "float32"),
+    "ws": ("sbuf", [D, D], "float32"),
+    "ys": ("sbuf", [D, D], "float32"),
+    "gp": ("psum", [D, 512], "float32"),
+    "g2p": ("psum", [D, 512], "float32"),
+    "wp": ("psum", [D, 512], "float32"),
+    "yp": ("psum", [D, 512], "float32"),
+}
+SEMAPHORES = ["ldx", "ldt", "cs", "m0", "own", "sc", "pr", "ac", "gok", "m1", "g2ok", "m2", "wok", "m3", "yok", "st",
+              "sent"] + ["arr%d" % k for k in range(NCHIPS)]
+
+
+def _engines(mask):
+    return bin(mask).count("1")
+
+
+def _plan(ranks, topo):
+    chips = sorted({topo.chip(c) for c in ranks})
+    every = range(topo.CHIPS * topo.CORES_PER_CHIP)
+    send, feed = {}, {}
+    for ci, ch in enumerate(chips):
+        share = {}
+        for r in sorted(c for c in ranks if topo.chip(c) == ch):
+            die = topo.die(r)
+            targets = [t for t in ranks if topo.chip(t) != ch and topo.die(t) == die]
+            targets.sort(key=lambda t: (chips.index(topo.chip(t)) - ci) % len(chips))
+            spare = [c for c in every if topo.chip(c) == ch and topo.die(c) == die and c not in ranks]
+            spare.sort(key=lambda s: -sum(topo.may_write(s, t) for t in targets))
+            team = [r] + spare[:HELPERS]
+            left = len(targets) - RANK_SHARE
+            share[r] = RANK_SHARE
+            for k, h in enumerate(team[1:]):
+                share[h] = -(-left // (len(team) - 1 - k))
+                left -= share[h]
+            free = list(targets)
+            for s in sorted(team, key=lambda s: sum(topo.may_write(s, t) for t in targets)):
+                can = sorted((t for t in free if topo.may_write(s, t)),
+                             key=lambda t: sum(topo.may_write(o, t) for o in team))[:share[s]]
+                send[s] = [t for t in targets if t in can]
+                free = [t for t in free if t not in can]
+            assert not free
+        feed[ch] = sorted(share, key=lambda s: (s in ranks, -share[s]))
+    return chips, send, feed
+
+
+def _ids(cores, topo):
+    return [DstId(rid=topo.addr(c)[0], pnc=topo.addr(c)[1]) for c in cores]
+
+
+def rank_program(g, core, T, topo):
+    ranks = list(T.cores)
+    chips, send, feed = _plan(ranks, topo)
+    if core not in send:
+        return
+    S = T.sem
+    ch = topo.chip(core)
+    ci = chips.index(ch)
+    home = sorted(c for c in ranks if topo.chip(c) == ch)
+    halves = [T.pair[:, k * D:(k + 1) * D] for k in range(len(home))]
+    slot = [T.land[:, k * D:(k + 1) * D] for k in range(NCHIPS)]
+
+    def fold_out():
+        to = send[core]
+        mask = topo.mask(core, to[0])
+        g.remote_dma_fused([RemoteDMATransfer(dst_ids=_ids(to, topo), dma_engine_mask=mask, remote_sem=S["arr%d" % ci],
+                                              srcs=halves, dsts=[slot[ci]] * len(to), alu_op=1)], local_sem=S.sent)
+        return _engines(mask)
+
+    if core not in ranks:
+        g.wait_ge(S.pr, sum(_engines(topo.mask(r, core)) for r in home))
+        g.wait_ge(S.sent, fold_out())
+        return
+
+    me = home.index(core)
+    mate = home[1 - me]
+    t, v = g.tensor, g.vector
+    cst = [T.cst[:, k * D:(k + 1) * D] for k in range(5)]
+    sx = [T.sx[:, k * D:(k + 1) * D] for k in range(5)]
+    gp, g2p, wp, yp = T.gp[:, 0:D], T.g2p[:, 0:D], T.wp[:, 0:D], T.yp[:, 0:D]
+
+    g.sync.dma_start(T.xs[:], T.x[:]).then_inc(S.ldx, 16)
+    g.scalar.wait_ge(S.ldx, 16)
+    g.scalar.dma_start(T.xts[:], T.xt[:]).then_inc(S.ldt, 16)
+
+    for k in range(5):
+        v.memset(cst[k], COEF[k]).then_inc(S.cs, 1)
+    t.wait_ge(S.ldx, 16)
+    t.matmul(gp, T.xs[:], T.xs[:], True, True).then_inc(S.m0, 1)
+    v.wait_ge(S.m0, 1)
+    v.tensor_copy(halves[me], gp).then_inc(S.own, 1)
+
+    peers = [s for s in feed[ch] if s != core]
+    mask1 = topo.mask(core, peers[0])
+    g.wait_ge(S.own, 1)
+    g.remote_dma_fused([RemoteDMATransfer(dst_ids=_ids(peers, topo), dma_engine_mask=mask1, remote_sem=S.pr,
+                                          srcs=[halves[me]], dsts=[halves[me]] * len(peers), alu_op=0)],
+                       local_sem=S.sent)
+    got = _engines(topo.mask(mate, core))
+    g.wait_ge(S.pr, got)
+    g.wait_ge(S.sent, _engines(mask1) + fold_out())
+
+    v.wait_ge(S.cs, 5)
+    v.wait_ge(S.ldx, 16)
+    v.wait_ge(S.ldt, 16)
+    for k in range(5):
+        v.tensor_tensor(sx[k], T.xs[:] if k == 0 else T.xts[:], cst[k], AluOpType.mult).then_inc(S.sc, 1)
+
+    def due(k):
+        s = [s for s in feed[chips[k]] if core in send[s]][0]
+        return feed[chips[k]].index(s) + 2 * send[s].index(core)
+    order = sorted((k for k in range(len(chips)) if k != ci), key=due)
+    v.wait_ge(S.pr, got)
+    v.tensor_tensor(gp, gp, halves[1 - me], AluOpType.add).then_inc(S.ac, 1)
+    for n, k in enumerate(order):
+        src = [s for s in feed[chips[k]] if core in send[s]][0]
+        v.wait_ge(S["arr%d" % k], _engines(topo.mask(src, core)))
+        v.wait_ge(S.ac, n + 1)
+        if n + 1 < len(order):
+            v.tensor_tensor(gp, gp, slot[k], AluOpType.add).then_inc(S.ac, 1)
+        else:
+            v.tensor_tensor(T.gs[:], gp, slot[k], AluOpType.add).then_inc(S.gok, 1)
+
+    t.wait_ge(S.gok, 1)
+    t.matmul(g2p, T.gs[:], T.gs[:], True, True).then_inc(S.m1, 1)
+    t.wait_ge(S.sc, 5)
+    t.matmul(wp, T.gs[:], sx[3], True, False)
+    v.wait_ge(S.m1, 1)
+    v.tensor_copy(T.g2s[:], g2p).then_inc(S.g2ok, 1)
+    t.wait_ge(S.g2ok, 1)
+    t.matmul(wp, T.g2s[:], sx[4], False, True).then_inc(S.m2, 1)
+    t.matmul(yp, sx[1], T.gs[:], True, False)
+    v.wait_ge(S.m2, 1)
+    v.wait_ge(S.sc, 5)
+    v.tensor_tensor(T.ws[:], wp, sx[2], AluOpType.add).then_inc(S.wok, 1)
+    t.wait_ge(S.wok, 1)
+    t.matmul(yp, T.ws[:], T.g2s[:], False, True).then_inc(S.m3, 1)
+    v.wait_ge(S.m3, 1)
+    v.tensor_tensor(T.ys[:], yp, sx[0], AluOpType.add).then_inc(S.yok, 1)
+    g.sync.wait_ge(S.yok, 1)
+    g.sync.dma_start(T.y[:], T.ys[:]).then_inc(S.st, 16)
+    g.sync.wait_ge(S.st, 16)

@@ -2,7 +2,8 @@ from concourse.bass import DstId, RemoteDMATransfer
 from concourse.mybir import AluOpType
 
 D = 128
-COEF = (2.25, -2.4375, 1.6875, -0.5625, 0.0625)
+H = D // 2
+A0, C1, W0, W2, RHO = 2.25, -0.5390625, 0.421875, 0.0625, -4.5
 HELPERS = 2
 RANK_SHARE = 2
 NCHIPS = 8
@@ -11,20 +12,23 @@ SCRATCH = {
     "xs": ("sbuf", [D, D], "float32"),
     "xts": ("sbuf", [D, D], "float32"),
     "cst": ("sbuf", [D, 5 * D], "float32"),
-    "sx": ("sbuf", [D, 5 * D], "float32"),
+    "sx": ("sbuf", [D, 4 * D], "float32"),
     "pair": ("sbuf", [D, 2 * D], "float32"),
-    "land": ("sbuf", [D, NCHIPS * D], "float32"),
+    "pc": ("sbuf", [D, H], "float32"),
+    "land": ("sbuf", [D, NCHIPS * H], "float32"),
     "gs": ("sbuf", [D, D], "float32"),
-    "g2s": ("sbuf", [D, D], "float32"),
+    "rg": ("sbuf", [D, D], "float32"),
+    "rs": ("sbuf", [D, D], "float32"),
     "ws": ("sbuf", [D, D], "float32"),
     "ys": ("sbuf", [D, D], "float32"),
     "gp": ("psum", [D, 512], "float32"),
     "g2p": ("psum", [D, 512], "float32"),
     "wp": ("psum", [D, 512], "float32"),
-    "yp": ("psum", [D, 512], "float32"),
+    "ypa": ("psum", [D, 512], "float32"),
+    "ypb": ("psum", [D, 512], "float32"),
 }
-SEMAPHORES = ["ldx", "ldt", "cs", "m0", "own", "sc", "pr", "ac", "gok", "m1", "g2ok", "m2", "wok", "m3", "yok", "st",
-              "sent"] + ["arr%d" % k for k in range(NCHIPS)]
+SEMAPHORES = ["ldx", "ldt", "cs", "m0", "own", "sc", "pr", "pcok", "ac", "gok", "fin", "rgok", "m1", "rok", "m2", "wok",
+              "m3a", "m3b", "yok", "st", "sent"] + ["arr%d" % k for k in range(NCHIPS)]
 
 
 def _engines(mask):
@@ -73,86 +77,116 @@ def rank_program(g, core, T, topo):
     ch = topo.chip(core)
     ci = chips.index(ch)
     home = sorted(c for c in ranks if topo.chip(c) == ch)
-    halves = [T.pair[:, k * D:(k + 1) * D] for k in range(len(home))]
-    slot = [T.land[:, k * D:(k + 1) * D] for k in range(NCHIPS)]
+    half = [k for k, r in enumerate(home) if topo.die(r) == topo.die(core)][0]
+    slot = [T.land[:, k * H:(k + 1) * H] for k in range(NCHIPS)]
+    t, v = g.tensor, g.vector
 
-    def fold_out():
-        to = send[core]
-        mask = topo.mask(core, to[0])
-        g.remote_dma_fused([RemoteDMATransfer(dst_ids=_ids(to, topo), dma_engine_mask=mask, remote_sem=S["arr%d" % ci],
-                                              srcs=halves, dsts=[slot[ci]] * len(to), alu_op=1)], local_sem=S.sent)
+    def piece(r, h):
+        return T.pair[:, r * D + h * H:r * D + (h + 1) * H]
+
+    def transfer(src, dst, to, sem, mask):
+        return RemoteDMATransfer(dst_ids=_ids(to, topo), dma_engine_mask=mask, remote_sem=sem,
+                                 srcs=[src], dsts=[dst] * len(to), alu_op=0)
+
+    def step2():
+        mask = topo.mask(core, send[core][0])
+        g.remote_dma_fused([transfer(T.pc[:], slot[ci], send[core], S["arr%d" % ci], mask)], local_sem=S.sent)
         return _engines(mask)
 
+    def split(mask):
+        bits = [b for b in range(mask.bit_length()) if (mask >> b) & 1]
+        n = len(bits) // 2
+        return [sum(1 << b for b in bits[:n]), sum(1 << b for b in bits[n:])]
+
     if core not in ranks:
-        g.wait_ge(S.pr, sum(_engines(topo.mask(r, core)) for r in home))
-        g.wait_ge(S.sent, fold_out())
+        v.wait_ge(S.pr, sum(_engines(split(topo.mask(r, core))[0]) for r in home))
+        v.tensor_tensor(T.pc[:], piece(0, half), piece(1, half), AluOpType.add).then_inc(S.pcok, 1)
+        g.wait_ge(S.pcok, 1)
+        g.wait_ge(S.sent, step2())
         return
 
-    me = home.index(core)
+    me = half
     mate = home[1 - me]
-    t, v = g.tensor, g.vector
     cst = [T.cst[:, k * D:(k + 1) * D] for k in range(5)]
-    sx = [T.sx[:, k * D:(k + 1) * D] for k in range(5)]
-    gp, g2p, wp, yp = T.gp[:, 0:D], T.g2p[:, 0:D], T.wp[:, 0:D], T.yp[:, 0:D]
+    sx = [T.sx[:, k * D:(k + 1) * D] for k in range(4)]
+    g2p, wp = T.g2p[:, 0:D], T.wp[:, 0:D]
+    gph = T.gp[:, me * H:(me + 1) * H]
+    gsh = T.gs[:, me * H:(me + 1) * H]
+    yp = [T.ypa[:, 0:H], T.ypb[:, 0:H]]
 
     g.sync.dma_start(T.xs[:], T.x[:]).then_inc(S.ldx, 16)
     g.scalar.wait_ge(S.ldx, 16)
     g.scalar.dma_start(T.xts[:], T.xt[:]).then_inc(S.ldt, 16)
 
-    for k in range(5):
-        v.memset(cst[k], COEF[k]).then_inc(S.cs, 1)
+    for k, a in enumerate((A0, C1, W0, W2, RHO)):
+        v.memset(cst[k], a).then_inc(S.cs, 1)
     t.wait_ge(S.ldx, 16)
-    t.matmul(gp, T.xs[:], T.xs[:], True, True).then_inc(S.m0, 1)
+    t.matmul(T.gp[:, 0:D], T.xs[:], T.xs[:], True, True).then_inc(S.m0, 1)
     v.wait_ge(S.m0, 1)
-    v.tensor_copy(halves[me], gp).then_inc(S.own, 1)
+    v.tensor_copy(T.pair[:, me * D:(me + 1) * D], T.gp[:, 0:D]).then_inc(S.own, 1)
 
-    peers = [s for s in feed[ch] if s != core]
-    mask1 = topo.mask(core, peers[0])
+    masks = split(topo.mask(core, mate))
     g.wait_ge(S.own, 1)
-    g.remote_dma_fused([RemoteDMATransfer(dst_ids=_ids(peers, topo), dma_engine_mask=mask1, remote_sem=S.pr,
-                                          srcs=[halves[me]], dsts=[halves[me]] * len(peers), alu_op=0)],
-                       local_sem=S.sent)
-    got = _engines(topo.mask(mate, core))
-    g.wait_ge(S.pr, got)
-    g.wait_ge(S.sent, _engines(mask1) + fold_out())
+    g.remote_dma_fused([transfer(piece(me, h), piece(me, h),
+                                 [s for s in feed[ch] if s != core and topo.die(s) == topo.die(home[h])], S.pr, masks[h])
+                        for h in range(len(home))], local_sem=S.sent)
+    left = sum(_engines(m) for m in masks)
+    g.wait_ge(S.pcok, 1)
+    left += step2()
+    g.wait_ge(S.gok, 1)
+    mask3 = topo.mask(core, mate)
+    g.remote_dma_fused([transfer(gsh, gsh, [mate], S.fin, mask3)], local_sem=S.sent)
+    g.wait_ge(S.sent, left + _engines(mask3))
 
     v.wait_ge(S.cs, 5)
     v.wait_ge(S.ldx, 16)
     v.wait_ge(S.ldt, 16)
-    for k in range(5):
+    for k in range(4):
         v.tensor_tensor(sx[k], T.xs[:] if k == 0 else T.xts[:], cst[k], AluOpType.mult).then_inc(S.sc, 1)
+
+    v.wait_ge(S.pr, _engines(split(topo.mask(mate, core))[me]))
+    v.tensor_tensor(T.pc[:], gph, piece(1 - me, me), AluOpType.add).then_inc(S.pcok, 1)
+    v.wait_ge(S.pcok, 1)
+    v.tensor_tensor(gph, gph, piece(1 - me, me), AluOpType.add).then_inc(S.ac, 1)
 
     def due(k):
         s = [s for s in feed[chips[k]] if core in send[s]][0]
         return feed[chips[k]].index(s) + 2 * send[s].index(core)
     order = sorted((k for k in range(len(chips)) if k != ci), key=due)
-    v.wait_ge(S.pr, got)
-    v.tensor_tensor(gp, gp, halves[1 - me], AluOpType.add).then_inc(S.ac, 1)
     for n, k in enumerate(order):
         src = [s for s in feed[chips[k]] if core in send[s]][0]
         v.wait_ge(S["arr%d" % k], _engines(topo.mask(src, core)))
         v.wait_ge(S.ac, n + 1)
         if n + 1 < len(order):
-            v.tensor_tensor(gp, gp, slot[k], AluOpType.add).then_inc(S.ac, 1)
+            v.tensor_tensor(gph, gph, slot[k], AluOpType.add).then_inc(S.ac, 1)
         else:
-            v.tensor_tensor(T.gs[:], gp, slot[k], AluOpType.add).then_inc(S.gok, 1)
+            v.tensor_tensor(gsh, gph, slot[k], AluOpType.add).then_inc(S.gok, 1)
 
+    whole = _engines(topo.mask(mate, core))
     t.wait_ge(S.gok, 1)
+    t.wait_ge(S.fin, whole)
     t.matmul(g2p, T.gs[:], T.gs[:], True, True).then_inc(S.m1, 1)
-    t.wait_ge(S.sc, 5)
-    t.matmul(wp, T.gs[:], sx[3], True, False)
+    v.wait_ge(S.gok, 1)
+    v.wait_ge(S.fin, whole)
+    v.tensor_tensor(T.rg[:], T.gs[:], cst[4], AluOpType.mult).then_inc(S.rgok, 1)
+    v.wait_ge(S.rgok, 1)
     v.wait_ge(S.m1, 1)
-    v.tensor_copy(T.g2s[:], g2p).then_inc(S.g2ok, 1)
-    t.wait_ge(S.g2ok, 1)
-    t.matmul(wp, T.g2s[:], sx[4], False, True).then_inc(S.m2, 1)
-    t.matmul(yp, sx[1], T.gs[:], True, False)
+    v.tensor_tensor(T.rs[:], g2p, T.rg[:], AluOpType.add).then_inc(S.rok, 1)
+    t.wait_ge(S.sc, 4)
+    t.matmul(yp[0], sx[1], T.gs[:, 0:H], True, False)
+    t.wait_ge(S.rok, 1)
+    t.matmul(wp, T.rs[:], sx[3], True, True).then_inc(S.m2, 1)
+    t.matmul(yp[1], sx[1], T.gs[:, H:D], True, False)
     v.wait_ge(S.m2, 1)
-    v.wait_ge(S.sc, 5)
+    v.wait_ge(S.sc, 4)
     v.tensor_tensor(T.ws[:], wp, sx[2], AluOpType.add).then_inc(S.wok, 1)
     t.wait_ge(S.wok, 1)
-    t.matmul(yp, T.ws[:], T.g2s[:], False, True).then_inc(S.m3, 1)
-    v.wait_ge(S.m3, 1)
-    v.tensor_tensor(T.ys[:], yp, sx[0], AluOpType.add).then_inc(S.yok, 1)
-    g.sync.wait_ge(S.yok, 1)
+    t.matmul(yp[0], T.ws[:], T.rs[:, 0:H], False, True).then_inc(S.m3a, 1)
+    t.matmul(yp[1], T.ws[:], T.rs[:, H:D], False, True).then_inc(S.m3b, 1)
+    v.wait_ge(S.m3a, 1)
+    v.tensor_tensor(T.ys[:, 0:H], yp[0], T.sx[:, 0:H], AluOpType.add).then_inc(S.yok, 1)
+    v.wait_ge(S.m3b, 1)
+    v.tensor_tensor(T.ys[:, H:D], yp[1], T.sx[:, H:D], AluOpType.add).then_inc(S.yok, 1)
+    g.sync.wait_ge(S.yok, 2)
     g.sync.dma_start(T.y[:], T.ys[:]).then_inc(S.st, 16)
     g.sync.wait_ge(S.st, 16)

@@ -3,7 +3,8 @@ from concourse.mybir import AluOpType
 
 D = 128
 H = D // 2
-A0, C1, W0, W2, RHO = 2.25, -0.5390625, 0.421875, 0.0625, -4.5
+SHIFT, AQ = -3.0, 0.0625
+B1, B2, C2 = -1.6128878593444824, 4.612887859344482, 7.440070629119873
 HELPERS = 2
 RANK_SHARE = 2
 NCHIPS = 8
@@ -11,24 +12,30 @@ NCHIPS = 8
 SCRATCH = {
     "xs": ("sbuf", [D, D], "float32"),
     "xts": ("sbuf", [D, D], "float32"),
-    "cst": ("sbuf", [D, 5 * D], "float32"),
-    "sx": ("sbuf", [D, 4 * D], "float32"),
+    "cm3": ("sbuf", [D, H], "float32"),
+    "e3": ("sbuf", [D, H], "float32"),
+    "sxa": ("sbuf", [D, D], "float32"),
+    "sxc": ("sbuf", [D, D], "float32"),
     "pair": ("sbuf", [D, 2 * D], "float32"),
     "pc": ("sbuf", [D, H], "float32"),
     "land": ("sbuf", [D, NCHIPS * H], "float32"),
     "gs": ("sbuf", [D, D], "float32"),
-    "rg": ("sbuf", [D, D], "float32"),
-    "rs": ("sbuf", [D, D], "float32"),
+    "ta": ("sbuf", [D, D], "float32"),
+    "tb": ("sbuf", [D, D], "float32"),
+    "qa": ("sbuf", [D, D], "float32"),
+    "qb": ("sbuf", [D, D], "float32"),
     "ws": ("sbuf", [D, D], "float32"),
     "ys": ("sbuf", [D, D], "float32"),
-    "gp": ("psum", [D, 512], "float32"),
+    "gpa": ("psum", [D, 512], "float32"),
+    "gpb": ("psum", [D, 512], "float32"),
     "g2p": ("psum", [D, 512], "float32"),
     "wp": ("psum", [D, 512], "float32"),
     "ypa": ("psum", [D, 512], "float32"),
     "ypb": ("psum", [D, 512], "float32"),
 }
-SEMAPHORES = ["ldx", "ldt", "cs", "m0", "own", "sc", "pr", "pcok", "ac", "gok", "fin", "rgok", "m1", "rok", "m2", "wok",
-              "m3a", "m3b", "yok", "st", "sent"] + ["arr%d" % k for k in range(NCHIPS)]
+SEMAPHORES = ["ldx", "ldt", "on1", "idok", "vq", "m0a", "m0b", "owna", "ownb", "sc", "pr", "pcok", "ac", "gok", "fin",
+              "m1", "r1", "r2", "m2", "wok", "m3a", "m3b", "yoka", "yokb", "sta", "stb",
+              "sent"] + ["arr%d" % k for k in range(NCHIPS)]
 
 
 def _engines(mask):
@@ -80,6 +87,7 @@ def rank_program(g, core, T, topo):
     half = [k for k, r in enumerate(home) if topo.die(r) == topo.die(core)][0]
     slot = [T.land[:, k * H:(k + 1) * H] for k in range(NCHIPS)]
     t, v = g.tensor, g.vector
+    add, mult = AluOpType.add, AluOpType.mult
 
     def piece(r, h):
         return T.pair[:, r * D + h * H:r * D + (h + 1) * H]
@@ -100,36 +108,46 @@ def rank_program(g, core, T, topo):
 
     if core not in ranks:
         v.wait_ge(S.pr, sum(_engines(split(topo.mask(r, core))[0]) for r in home))
-        v.tensor_tensor(T.pc[:], piece(0, half), piece(1, half), AluOpType.add).then_inc(S.pcok, 1)
+        v.tensor_tensor(T.pc[:], piece(0, half), piece(1, half), add).then_inc(S.pcok, 1)
         g.wait_ge(S.pcok, 1)
         g.wait_ge(S.sent, step2())
         return
 
     me = half
-    mate = home[1 - me]
-    cst = [T.cst[:, k * D:(k + 1) * D] for k in range(5)]
-    sx = [T.sx[:, k * D:(k + 1) * D] for k in range(4)]
+    oth = 1 - me
+    mate = home[oth]
+
+    def cols(buf, h):
+        return buf[:, h * H:(h + 1) * H]
+
+    gpo = T.gpa[:, 0:H]
+    gph = T.gpb[:, 0:H]
+    gsh = cols(T.gs, me)
     g2p, wp = T.g2p[:, 0:D], T.wp[:, 0:D]
-    gph = T.gp[:, me * H:(me + 1) * H]
-    gsh = T.gs[:, me * H:(me + 1) * H]
     yp = [T.ypa[:, 0:H], T.ypb[:, 0:H]]
 
     g.sync.dma_start(T.xs[:], T.x[:]).then_inc(S.ldx, 16)
     g.scalar.wait_ge(S.ldx, 16)
     g.scalar.dma_start(T.xts[:], T.xt[:]).then_inc(S.ldt, 16)
 
-    for k, a in enumerate((A0, C1, W0, W2, RHO)):
-        v.memset(cst[k], a).then_inc(S.cs, 1)
+    v.memset(T.cm3[:], SHIFT).then_inc(S.on1, 1)
+    g.wait_ge(S.on1, 1)
+    g.affine_select(T.e3[:], T.cm3[:], [[-1, H]], AluOpType.is_equal, 0.0, -me * H, 1).then_inc(S.idok, 1)
+
     t.wait_ge(S.ldx, 16)
-    t.matmul(T.gp[:, 0:D], T.xs[:], T.xs[:], True, True).then_inc(S.m0, 1)
-    v.wait_ge(S.m0, 1)
-    v.tensor_copy(T.pair[:, me * D:(me + 1) * D], T.gp[:, 0:D]).then_inc(S.own, 1)
+    t.matmul(gpo, T.xs[:], cols(T.xs, oth), True, True).then_inc(S.m0a, 1)
+    t.matmul(gph, T.xs[:], cols(T.xs, me), True, True).then_inc(S.m0b, 1)
+    v.wait_ge(S.m0a, 1)
+    v.tensor_copy(piece(me, oth), gpo).then_inc(S.owna, 1)
+    v.wait_ge(S.m0b, 1)
+    v.tensor_copy(piece(me, me), gph).then_inc(S.ownb, 1)
 
     masks = split(topo.mask(core, mate))
-    g.wait_ge(S.own, 1)
-    g.remote_dma_fused([transfer(piece(me, h), piece(me, h),
-                                 [s for s in feed[ch] if s != core and topo.die(s) == topo.die(home[h])], S.pr, masks[h])
-                        for h in range(len(home))], local_sem=S.sent)
+    for h, ready in ((oth, S.owna), (me, S.ownb)):
+        g.wait_ge(ready, 1)
+        g.remote_dma_fused([transfer(piece(me, h), piece(me, h),
+                                     [s for s in feed[ch] if s != core and topo.die(s) == topo.die(home[h])],
+                                     S.pr, masks[h])], local_sem=S.sent)
     left = sum(_engines(m) for m in masks)
     g.wait_ge(S.pcok, 1)
     left += step2()
@@ -138,55 +156,63 @@ def rank_program(g, core, T, topo):
     g.remote_dma_fused([transfer(gsh, gsh, [mate], S.fin, mask3)], local_sem=S.sent)
     g.wait_ge(S.sent, left + _engines(mask3))
 
-    v.wait_ge(S.cs, 5)
-    v.wait_ge(S.ldx, 16)
     v.wait_ge(S.ldt, 16)
-    for k in range(4):
-        v.tensor_tensor(sx[k], T.xs[:] if k == 0 else T.xts[:], cst[k], AluOpType.mult).then_inc(S.sc, 1)
+    v.tensor_scalar(T.sxa[:], T.xts[:], AQ, None, mult).then_inc(S.sc, 1)
+    v.tensor_scalar(T.sxc[:], T.xts[:], AQ * C2, None, mult).then_inc(S.sc, 1)
 
     v.wait_ge(S.pr, _engines(split(topo.mask(mate, core))[me]))
-    v.tensor_tensor(T.pc[:], gph, piece(1 - me, me), AluOpType.add).then_inc(S.pcok, 1)
+    v.tensor_tensor(T.pc[:], gph, piece(oth, me), add).then_inc(S.pcok, 1)
     v.wait_ge(S.pcok, 1)
-    v.tensor_tensor(gph, gph, piece(1 - me, me), AluOpType.add).then_inc(S.ac, 1)
+    v.tensor_tensor(gph, gph, piece(oth, me), add).then_inc(S.ac, 1)
+    v.wait_ge(S.ac, 1)
+    v.wait_ge(S.idok, 1)
+    v.tensor_tensor(gph, gph, T.e3[:], add).then_inc(S.ac, 1)
 
     def due(k):
         s = [s for s in feed[chips[k]] if core in send[s]][0]
-        return feed[chips[k]].index(s) + 2 * send[s].index(core)
+        return (s not in ranks, feed[chips[k]].index(s) + send[s].index(core))
     order = sorted((k for k in range(len(chips)) if k != ci), key=due)
     for n, k in enumerate(order):
         src = [s for s in feed[chips[k]] if core in send[s]][0]
         v.wait_ge(S["arr%d" % k], _engines(topo.mask(src, core)))
-        v.wait_ge(S.ac, n + 1)
+        v.wait_ge(S.ac, n + 2)
         if n + 1 < len(order):
-            v.tensor_tensor(gph, gph, slot[k], AluOpType.add).then_inc(S.ac, 1)
+            v.tensor_tensor(gph, gph, slot[k], add).then_inc(S.ac, 1)
         else:
-            v.tensor_tensor(gsh, gph, slot[k], AluOpType.add).then_inc(S.gok, 1)
+            v.tensor_tensor(gsh, gph, slot[k], add).then_inc(S.gok, 1)
 
     whole = _engines(topo.mask(mate, core))
     t.wait_ge(S.gok, 1)
     t.wait_ge(S.fin, whole)
     t.matmul(g2p, T.gs[:], T.gs[:], True, True).then_inc(S.m1, 1)
     v.wait_ge(S.gok, 1)
+    v.tensor_scalar(cols(T.ta, me), gsh, B2, None, mult).then_inc(S.vq, 1)
+    v.tensor_scalar(cols(T.tb, me), gsh, B1, None, mult).then_inc(S.vq, 1)
     v.wait_ge(S.fin, whole)
-    v.tensor_tensor(T.rg[:], T.gs[:], cst[4], AluOpType.mult).then_inc(S.rgok, 1)
-    v.wait_ge(S.rgok, 1)
+    v.tensor_scalar(cols(T.ta, oth), cols(T.gs, oth), B2, None, mult).then_inc(S.vq, 1)
+    v.tensor_scalar(cols(T.tb, oth), cols(T.gs, oth), B1, None, mult).then_inc(S.vq, 1)
+    v.wait_ge(S.vq, 4)
     v.wait_ge(S.m1, 1)
-    v.tensor_tensor(T.rs[:], g2p, T.rg[:], AluOpType.add).then_inc(S.rok, 1)
-    t.wait_ge(S.sc, 4)
-    t.matmul(yp[0], sx[1], T.gs[:, 0:H], True, False)
-    t.wait_ge(S.rok, 1)
-    t.matmul(wp, T.rs[:], sx[3], True, True).then_inc(S.m2, 1)
-    t.matmul(yp[1], sx[1], T.gs[:, H:D], True, False)
+    v.tensor_tensor(T.qa[:], g2p, T.ta[:], add).then_inc(S.r1, 1)
+    v.tensor_tensor(T.qb[:], g2p, T.tb[:], add).then_inc(S.r2, 1)
+    t.wait_ge(S.sc, 2)
+    t.wait_ge(S.r1, 1)
+    t.matmul(wp, T.qa[:], T.sxa[:], True, True).then_inc(S.m2, 1)
     v.wait_ge(S.m2, 1)
-    v.wait_ge(S.sc, 4)
-    v.tensor_tensor(T.ws[:], wp, sx[2], AluOpType.add).then_inc(S.wok, 1)
+    v.wait_ge(S.sc, 2)
+    v.tensor_tensor(T.ws[:], wp, T.sxc[:], add).then_inc(S.wok, 1)
     t.wait_ge(S.wok, 1)
-    t.matmul(yp[0], T.ws[:], T.rs[:, 0:H], False, True).then_inc(S.m3a, 1)
-    t.matmul(yp[1], T.ws[:], T.rs[:, H:D], False, True).then_inc(S.m3b, 1)
+    t.wait_ge(S.r2, 1)
+    t.matmul(yp[0], T.ws[:], cols(T.qb, 0), True, True).then_inc(S.m3a, 1)
+    t.matmul(yp[1], T.ws[:], cols(T.qb, 1), True, True).then_inc(S.m3b, 1)
     v.wait_ge(S.m3a, 1)
-    v.tensor_tensor(T.ys[:, 0:H], yp[0], T.sx[:, 0:H], AluOpType.add).then_inc(S.yok, 1)
+    v.tensor_copy(cols(T.ys, 0), yp[0]).then_inc(S.yoka, 1)
     v.wait_ge(S.m3b, 1)
-    v.tensor_tensor(T.ys[:, H:D], yp[1], T.sx[:, H:D], AluOpType.add).then_inc(S.yok, 1)
-    g.sync.wait_ge(S.yok, 2)
-    g.sync.dma_start(T.y[:], T.ys[:]).then_inc(S.st, 16)
-    g.sync.wait_ge(S.st, 16)
+    v.tensor_copy(cols(T.ys, 1), yp[1]).then_inc(S.yokb, 1)
+    g.sync.wait_ge(S.yoka, 1)
+    g.sync.dma_start(T.y[:, 0:H], cols(T.ys, 0)).then_inc(S.sta, 16)
+    g.scalar.wait_ge(S.ldt, 16)
+    g.scalar.wait_ge(S.yokb, 1)
+    g.scalar.dma_start(T.y[:, H:D], cols(T.ys, 1)).then_inc(S.stb, 16)
+    g.sync.wait_ge(S.sta, 16)
+    g.scalar.wait_ge(S.stb, 16)

from concourse.bass import DstId, RemoteDMATransfer
from concourse.mybir import AluOpType

D = 128
H = D // 2
SHIFT, AQ = -3.0, 0.0625
B1, B2, C2 = -1.6128878593444824, 4.612887859344482, 7.440070629119873
HELPERS = 2
RANK_SHARE = 2
NCHIPS = 8

SCRATCH = {
    "xs": ("sbuf", [D, D], "float32"),
    "xts": ("sbuf", [D, D], "float32"),
    "cm3": ("sbuf", [D, H], "float32"),
    "e3": ("sbuf", [D, H], "float32"),
    "sxa": ("sbuf", [D, D], "float32"),
    "sxc": ("sbuf", [D, D], "float32"),
    "pair": ("sbuf", [D, 2 * D], "float32"),
    "pc": ("sbuf", [D, H], "float32"),
    "land": ("sbuf", [D, NCHIPS * H], "float32"),
    "gs": ("sbuf", [D, D], "float32"),
    "ta": ("sbuf", [D, D], "float32"),
    "tb": ("sbuf", [D, D], "float32"),
    "qa": ("sbuf", [D, D], "float32"),
    "qb": ("sbuf", [D, D], "float32"),
    "ws": ("sbuf", [D, D], "float32"),
    "ys": ("sbuf", [D, D], "float32"),
    "gpa": ("psum", [D, 512], "float32"),
    "gpb": ("psum", [D, 512], "float32"),
    "g2p": ("psum", [D, 512], "float32"),
    "wp": ("psum", [D, 512], "float32"),
    "ypa": ("psum", [D, 512], "float32"),
    "ypb": ("psum", [D, 512], "float32"),
}
SEMAPHORES = ["ldx", "ldt", "on1", "idok", "vq", "m0a", "m0b", "owna", "ownb", "sc", "pr", "pcok", "ac", "gok", "fin",
              "m1", "r1", "r2", "m2", "wok", "m3a", "m3b", "yoka", "yokb", "sta", "stb",
              "sent"] + ["arr%d" % k for k in range(NCHIPS)]


def _engines(mask):
    return bin(mask).count("1")


def _plan(ranks, topo):
    chips = sorted({topo.chip(c) for c in ranks})
    every = range(topo.CHIPS * topo.CORES_PER_CHIP)
    send, feed = {}, {}
    for ci, ch in enumerate(chips):
        share = {}
        for r in sorted(c for c in ranks if topo.chip(c) == ch):
            die = topo.die(r)
            targets = [t for t in ranks if topo.chip(t) != ch and topo.die(t) == die]
            targets.sort(key=lambda t: (chips.index(topo.chip(t)) - ci) % len(chips))
            spare = [c for c in every if topo.chip(c) == ch and topo.die(c) == die and c not in ranks]
            spare.sort(key=lambda s: -sum(topo.may_write(s, t) for t in targets))
            team = [r] + spare[:HELPERS]
            left = len(targets) - RANK_SHARE
            share[r] = RANK_SHARE
            for k, h in enumerate(team[1:]):
                share[h] = -(-left // (len(team) - 1 - k))
                left -= share[h]
            free = list(targets)
            for s in sorted(team, key=lambda s: sum(topo.may_write(s, t) for t in targets)):
                can = sorted((t for t in free if topo.may_write(s, t)),
                             key=lambda t: sum(topo.may_write(o, t) for o in team))[:share[s]]
                send[s] = [t for t in targets if t in can]
                free = [t for t in free if t not in can]
            assert not free
        feed[ch] = sorted(share, key=lambda s: (s in ranks, -share[s]))
    return chips, send, feed


def _ids(cores, topo):
    return [DstId(rid=topo.addr(c)[0], pnc=topo.addr(c)[1]) for c in cores]


def rank_program(g, core, T, topo):
    ranks = list(T.cores)
    chips, send, feed = _plan(ranks, topo)
    if core not in send:
        return
    S = T.sem
    ch = topo.chip(core)
    ci = chips.index(ch)
    home = sorted(c for c in ranks if topo.chip(c) == ch)
    half = [k for k, r in enumerate(home) if topo.die(r) == topo.die(core)][0]
    slot = [T.land[:, k * H:(k + 1) * H] for k in range(NCHIPS)]
    t, v = g.tensor, g.vector
    add, mult = AluOpType.add, AluOpType.mult

    def piece(r, h):
        return T.pair[:, r * D + h * H:r * D + (h + 1) * H]

    def transfer(src, dst, to, sem, mask):
        return RemoteDMATransfer(dst_ids=_ids(to, topo), dma_engine_mask=mask, remote_sem=sem,
                                 srcs=[src], dsts=[dst] * len(to), alu_op=0)

    def step2():
        mask = topo.mask(core, send[core][0])
        g.remote_dma_fused([transfer(T.pc[:], slot[ci], send[core], S["arr%d" % ci], mask)], local_sem=S.sent)
        return _engines(mask)

    def split(mask):
        bits = [b for b in range(mask.bit_length()) if (mask >> b) & 1]
        n = len(bits) // 2
        return [sum(1 << b for b in bits[:n]), sum(1 << b for b in bits[n:])]

    if core not in ranks:
        v.wait_ge(S.pr, sum(_engines(split(topo.mask(r, core))[0]) for r in home))
        v.tensor_tensor(T.pc[:], piece(0, half), piece(1, half), add).then_inc(S.pcok, 1)
        g.wait_ge(S.pcok, 1)
        g.wait_ge(S.sent, step2())
        return

    me = half
    oth = 1 - me
    mate = home[oth]

    def cols(buf, h):
        return buf[:, h * H:(h + 1) * H]

    gpo = T.gpa[:, 0:H]
    gph = T.gpb[:, 0:H]
    gsh = cols(T.gs, me)
    g2p, wp = T.g2p[:, 0:D], T.wp[:, 0:D]
    yp = [T.ypa[:, 0:H], T.ypb[:, 0:H]]

    g.sync.dma_start(T.xs[:], T.x[:]).then_inc(S.ldx, 16)
    g.scalar.wait_ge(S.ldx, 16)
    g.scalar.dma_start(T.xts[:], T.xt[:]).then_inc(S.ldt, 16)

    v.memset(T.cm3[:], SHIFT).then_inc(S.on1, 1)
    g.wait_ge(S.on1, 1)
    g.affine_select(T.e3[:], T.cm3[:], [[-1, H]], AluOpType.is_equal, 0.0, -me * H, 1).then_inc(S.idok, 1)

    t.wait_ge(S.ldx, 16)
    t.matmul(gpo, T.xs[:], cols(T.xs, oth), True, True).then_inc(S.m0a, 1)
    t.matmul(gph, T.xs[:], cols(T.xs, me), True, True).then_inc(S.m0b, 1)
    v.wait_ge(S.m0a, 1)
    v.tensor_copy(piece(me, oth), gpo).then_inc(S.owna, 1)
    v.wait_ge(S.m0b, 1)
    v.tensor_copy(piece(me, me), gph).then_inc(S.ownb, 1)

    masks = split(topo.mask(core, mate))
    for h, ready in ((oth, S.owna), (me, S.ownb)):
        g.wait_ge(ready, 1)
        g.remote_dma_fused([transfer(piece(me, h), piece(me, h),
                                     [s for s in feed[ch] if s != core and topo.die(s) == topo.die(home[h])],
                                     S.pr, masks[h])], local_sem=S.sent)
    left = sum(_engines(m) for m in masks)
    g.wait_ge(S.pcok, 1)
    left += step2()
    g.wait_ge(S.gok, 1)
    mask3 = topo.mask(core, mate)
    g.remote_dma_fused([transfer(gsh, gsh, [mate], S.fin, mask3)], local_sem=S.sent)
    g.wait_ge(S.sent, left + _engines(mask3))

    v.wait_ge(S.ldt, 16)
    v.tensor_scalar(T.sxa[:], T.xts[:], AQ, None, mult).then_inc(S.sc, 1)
    v.tensor_scalar(T.sxc[:], T.xts[:], AQ * C2, None, mult).then_inc(S.sc, 1)

    v.wait_ge(S.pr, _engines(split(topo.mask(mate, core))[me]))
    v.tensor_tensor(T.pc[:], gph, piece(oth, me), add).then_inc(S.pcok, 1)
    v.wait_ge(S.pcok, 1)
    v.tensor_tensor(gph, gph, piece(oth, me), add).then_inc(S.ac, 1)
    v.wait_ge(S.ac, 1)
    v.wait_ge(S.idok, 1)
    v.tensor_tensor(gph, gph, T.e3[:], add).then_inc(S.ac, 1)

    def due(k):
        s = [s for s in feed[chips[k]] if core in send[s]][0]
        return (s not in ranks, feed[chips[k]].index(s) + send[s].index(core))
    order = sorted((k for k in range(len(chips)) if k != ci), key=due)
    for n, k in enumerate(order):
        src = [s for s in feed[chips[k]] if core in send[s]][0]
        v.wait_ge(S["arr%d" % k], _engines(topo.mask(src, core)))
        v.wait_ge(S.ac, n + 2)
        if n + 1 < len(order):
            v.tensor_tensor(gph, gph, slot[k], add).then_inc(S.ac, 1)
        else:
            v.tensor_tensor(gsh, gph, slot[k], add).then_inc(S.gok, 1)

    whole = _engines(topo.mask(mate, core))
    t.wait_ge(S.gok, 1)
    t.wait_ge(S.fin, whole)
    t.matmul(g2p, T.gs[:], T.gs[:], True, True).then_inc(S.m1, 1)
    v.wait_ge(S.gok, 1)
    v.tensor_scalar(cols(T.ta, me), gsh, B2, None, mult).then_inc(S.vq, 1)
    v.tensor_scalar(cols(T.tb, me), gsh, B1, None, mult).then_inc(S.vq, 1)
    v.wait_ge(S.fin, whole)
    v.tensor_scalar(cols(T.ta, oth), cols(T.gs, oth), B2, None, mult).then_inc(S.vq, 1)
    v.tensor_scalar(cols(T.tb, oth), cols(T.gs, oth), B1, None, mult).then_inc(S.vq, 1)
    v.wait_ge(S.vq, 4)
    v.wait_ge(S.m1, 1)
    v.tensor_tensor(T.qa[:], g2p, T.ta[:], add).then_inc(S.r1, 1)
    v.tensor_tensor(T.qb[:], g2p, T.tb[:], add).then_inc(S.r2, 1)
    t.wait_ge(S.sc, 2)
    t.wait_ge(S.r1, 1)
    t.matmul(wp, T.qa[:], T.sxa[:], True, True).then_inc(S.m2, 1)
    v.wait_ge(S.m2, 1)
    v.wait_ge(S.sc, 2)
    v.tensor_tensor(T.ws[:], wp, T.sxc[:], add).then_inc(S.wok, 1)
    t.wait_ge(S.wok, 1)
    t.wait_ge(S.r2, 1)
    t.matmul(yp[0], T.ws[:], cols(T.qb, 0), True, True).then_inc(S.m3a, 1)
    t.matmul(yp[1], T.ws[:], cols(T.qb, 1), True, True).then_inc(S.m3b, 1)
    v.wait_ge(S.m3a, 1)
    v.tensor_copy(cols(T.ys, 0), yp[0]).then_inc(S.yoka, 1)
    v.wait_ge(S.m3b, 1)
    v.tensor_copy(cols(T.ys, 1), yp[1]).then_inc(S.yokb, 1)
    g.sync.wait_ge(S.yoka, 1)
    g.sync.dma_start(T.y[:, 0:H], cols(T.ys, 0)).then_inc(S.sta, 16)
    g.scalar.wait_ge(S.ldt, 16)
    g.scalar.wait_ge(S.yokb, 1)
    g.scalar.dma_start(T.y[:, H:D], cols(T.ys, 1)).then_inc(S.stb, 16)
    g.sync.wait_ge(S.sta, 16)
    g.scalar.wait_ge(S.stb, 16)
